import numpy as np
import ml_dtypes


def mxq(x, axis, fmt="e4m3"):
    dtype, down = {"e4m3": (ml_dtypes.float8_e4m3fn, 7), "e5m2": (ml_dtypes.float8_e5m2, 14)}[fmt]
    v = np.moveaxis(np.asarray(x, np.float32).astype(ml_dtypes.bfloat16).astype(np.float64), axis, -1)
    blocks = v.reshape(v.shape[:-1] + (-1, 32))
    amax = np.abs(blocks).max(-1, keepdims=True)
    byte = np.maximum(np.where(amax > 0, np.frexp(amax)[1] - 1 + 127, 0) - down, 1)
    scale = np.exp2(byte - 127.0)
    codes = (blocks / scale).astype(np.float32).astype(dtype).astype(np.float64)
    return np.moveaxis((codes * scale).reshape(v.shape), -1, axis)


WIDE = False


def mx_kscale(k):
    if not WIDE:
        return np.ones(k)
    levels = np.array([10, -10, 5, -5, 0])
    if k % 512:
        return np.exp2(np.random.permutation(np.resize(levels, k // 32))).repeat(32)
    a = np.empty((k // 512, 16))
    for p in range(k // 512):
        a[p, :8] = np.random.permutation(np.resize(levels, 8))
        for g in range(8):
            far = levels[np.abs(levels - a[p, g]) >= 10]
            a[p, g + 8] = far[np.random.randint(len(far))]
    return np.exp2(a.ravel()).repeat(32)


def f64(x):
    return np.asarray(x).astype(np.float64)


def striped(idx):
    return np.tile(idx.reshape(-1, 16).T, (8, 1)).astype(np.uint16)


def unstriped(offs):
    return offs[:16].T.reshape(-1).astype(np.int64)


def striped8(idx):
    return np.concatenate([x.reshape(-1, 16).T for x in idx]).astype(np.uint16)


def runs(offs, k):
    lists = np.stack([offs[16 * r : 16 * r + 16].T.reshape(-1) for r in range(8)]).astype(np.int64)
    return lists[np.arange(k) % 512 // 64]


def pack_weight(w):
    k, n = w.shape
    w = f64(np.asarray(w, np.float32).astype(ml_dtypes.bfloat16)).reshape(k // 32, 32, n)
    amax = np.abs(w).max(1)
    byte = np.clip(np.where(amax > 0, np.frexp(amax)[1] - 1 + 127 - 7, 1), 1, 254)
    scaled = (w * np.exp2(127.0 - byte)[:, None, :]).reshape(k, n).astype(np.float32)
    words = np.ascontiguousarray(scaled.reshape(k // 512, 128, 4, n).transpose(0, 1, 3, 2)).astype(ml_dtypes.float8_e4m3fn).view(np.uint8)
    return words, np.ascontiguousarray(byte.astype(np.uint8).reshape(k // 512, 16, n))


def unpack_weight(words, scales):
    g, p, n, _ = words.shape
    vals = np.ascontiguousarray(words).view(ml_dtypes.float8_e4m3fn).astype(np.float64) * np.repeat(np.exp2(scales.astype(np.float64) - 127.0), 8, axis=1)[..., None]
    return vals.transpose(0, 1, 3, 2).reshape(g * 512, n)


K, T, S, N, H = 512, 2048, 512, 512, 512


def setup_inputs():
    n = np.random.standard_normal
    s = mx_kscale(K)[:, None]
    u = mx_kscale(S)
    packed_xT = pack_weight(n((K, T)) * s)
    return {
        "x_words": packed_xT[0],
        "x_scales": packed_xT[1],
        "wa": (n((K, H)) / np.sqrt(K) / s).astype(np.float32),
        "gt": (np.random.uniform(0.5, 1.5, (S, 1)) * u[:, None]).astype(np.float32),
        "w1": (n((S, N)) / np.sqrt(S) / u[:, None]).astype(np.float32),
        "offs": striped(np.random.permutation(T)[:S]),
        "fl": striped8(np.stack([np.random.permutation(H) for _ in range(8)])),
    }


def reference(x_words, x_scales, wa, gt, w1, offs, fl):
    xq = unpack_weight(x_words, x_scales)[:, unstriped(offs)]
    y = xq.T @ mxq(f64(wa), 0, "e4m3")
    pw = (y) ** 2
    z = f64(gt) * ((y[np.arange(S)[:, None], runs(fl, S)]) * ((2.0 * pw) / (pw + pw[np.arange(S)[:, None], runs(fl, S)] + 0.25)))
    return mxq(f64(w1), 0, "e4m3").T @ mxq(z, 0, "e4m3")

@@ -1,0 +1,210 @@
+from contextlib import ExitStack
+
+import concourse.mybir as mybir
+
+K, T, S, N, H = 512, 2048, 512, 512, 512
+FLOPS = 2 * K * S * H + 2 * S * N * H
+
+F32 = mybir.dt.float32
+BF16 = mybir.dt.bfloat16
+I32 = mybir.dt.int32
+U32 = mybir.dt.uint32
+U16 = mybir.dt.uint16
+U8 = mybir.dt.uint8
+FP8X4 = mybir.dt.float8_e4m3fn_x4
+ACT = mybir.ActivationFunctionType
+ALU = mybir.AluOpType
+
+P = 128
+PACK = 4
+HALF = 256
+VECTOR_SHARE = 176
+PIECES = ((0, 256), (256, 128), (384, 128))
+
+
+def tile_picked_featnorm_none_p_kernel(tc, x_words, x_scales, wa, gt, w1, offs, fl, out):
+    nc = tc.nc
+    with ExitStack() as ctx:
+        keep = ctx.enter_context(tc.tile_pool(name="keep", bufs=1))
+        psum = ctx.enter_context(tc.psum_pool(name="psum", bufs=1))
+
+        def sb(shape, dtype, name):
+            return keep.tile(shape, dtype, name=name, align_bytes=64)
+
+        offs_sb = keep.tile([P, S // 16], U16, name="offs_sb")
+        fl_sb = keep.tile([P, H // 16], U16, name="fl_sb")
+        xw = sb([P, T], U32, "xw")
+        xs = sb([P, T], U8, "xs")
+        gw = sb([P, S], U32, "gw")
+        gs = sb([P, S], U8, "gs")
+        gate = sb([P, PACK], F32, "gate")
+        eighth = sb([P, 1], F32, "eighth")
+        wa_raw = [sb([P, PACK, HALF], F32, "wa_raw%d" % h) for h in range(2)]
+        w1_raw = [sb([P, PACK, HALF], F32, "w1_raw%d" % h) for h in range(2)]
+
+        nc.sync.dma_start(offs_sb[:], offs)
+        nc.vector.memset(xs[:].bitcast(I32), 0)
+        nc.vector.memset(eighth[:], 0.125)
+        scale_rows = x_scales[0].bitcast(I32).rearrange("(q r) c -> r q c", r=4)
+        for r in range(4):
+            nc.scalar.dma_start(xs[:].bitcast(I32)[r:P:32, :], scale_rows[r])
+        nc.sync.dma_start(xw[:].bitcast(I32), x_words[0].rearrange("p n t -> p (n t)").bitcast(I32))
+        wa_rows = wa.rearrange("(p j) n -> p j n", j=PACK)
+        w1_rows = w1.rearrange("(p j) n -> p j n", j=PACK)
+        for h in range(2):
+            nc.sync.dma_start(wa_raw[h][:], wa_rows[:, :, h * HALF : (h + 1) * HALF])
+        nc.sync.dma_start(gate[:], gt.rearrange("(p t) o -> p (t o)", t=PACK))
+        nc.sync.dma_start(fl_sb[:], fl)
+        for h in range(2):
+            nc.sync.dma_start(w1_raw[h][:], w1_rows[:, :, h * HALF : (h + 1) * HALF])
+
+        nc.vector.tensor_copy(gs[:].rearrange("p (t m) -> p m t", t=PACK), xs[:].indirect(offs_sb[:]))
+        nc.vector.tensor_copy(gw[:].rearrange("p (t m) -> p m t", t=PACK), xw[:].indirect(offs_sb[:]))
+
+        def woven(flat):
+            return flat.rearrange("p (c i t) -> p c t i", i=4, t=PACK)
+
+        def planes(stack):
+            return stack.rearrange("p t (c i) -> p c t i", i=4)
+
+        def cast(copy, grouped, raw, lo, hi):
+            copy(woven(grouped[:, PACK * lo : PACK * hi]), planes(raw[:, :, lo:hi]))
+
+        def quantize(grouped, width, name):
+            codes = sb([P, width], U32, name + "_codes")
+            scales = sb([P, width], U8, name + "_scales")
+            nc.vector.quantize_mx(out=codes[:].bitcast(FP8X4), scales=scales[:], in_=grouped[:])
+            return codes, scales
+
+        def half(h):
+            return slice(h * HALF, (h + 1) * HALF)
+
+        y_ps = [psum.tile([P, H], F32, name="y_ps%d" % t) for t in range(PACK)]
+        for h in range(2):
+            grouped = sb([P, PACK * HALF], BF16, "wa_bf%d" % h)
+            if h == 0:
+                cast(nc.scalar.copy, grouped, wa_raw[h], 0, HALF)
+            else:
+                cast(nc.vector.tensor_copy, grouped, wa_raw[h], 0, VECTOR_SHARE)
+                cast(nc.scalar.copy, grouped, wa_raw[h], VECTOR_SHARE, HALF)
+            codes, scales = quantize(grouped, HALF, "wa%d" % h)
+            for t in range(PACK):
+                cols = slice(t * P, (t + 1) * P)
+                nc.tensor.matmul_mx(
+                    out=y_ps[t][:, half(h)],
+                    lhsT=gw[:, cols].bitcast(FP8X4),
+                    lhsT_scale=gs[:, cols],
+                    rhs=codes[:].bitcast(FP8X4),
+                    rhs_scale=scales[:],
+                    start=True,
+                    stop=True,
+                )
+
+        gy = [sb([P, H], F32, "gy%d" % t) for t in range(PACK)]
+        pw = [sb([P, H], F32, "pw%d" % t) for t in range(PACK)]
+        num = [sb([P, PACK, HALF], F32, "num%d" % h) for h in range(2)]
+        pwf = [sb([P, PACK, HALF], F32, "pwf%d" % h) for h in range(2)]
+        den = [sb([P, PACK, HALF], F32, "den%d" % h) for h in range(2)]
+
+        def square_out(t):
+            nc.scalar.activation(pw[t][:], y_ps[t][:], ACT.Square)
+
+        def gate_out(t, engine):
+            if engine == "s":
+                nc.scalar.activation(gy[t][:], y_ps[t][:], ACT.Copy, scale=gate[:, t : t + 1])
+            else:
+                nc.vector.tensor_scalar(gy[t][:], y_ps[t][:], gate[:, t : t + 1], None, ALU.mult)
+
+        def entries(h):
+            return fl_sb[:, h * HALF // 16 : (h + 1) * HALF // 16]
+
+        def fetch_power(t, h):
+            nc.scalar.activation(pwf[h][:, t, :], pw[t][:].indirect(entries(h)), ACT.Copy)
+
+        def fetch_num(t, h):
+            nc.vector.tensor_tensor(num[h][:, t, :], gy[t][:].indirect(entries(h)), pw[t][:, half(h)], ALU.mult)
+
+        def add_den(t, h):
+            nc.vector.tensor_tensor(den[h][:, t, :], pwf[h][:, t, :], pw[t][:, half(h)], ALU.add)
+
+        recip = {}
+
+        def invert(piece):
+            lo, width = PIECES[piece]
+            h, at = divmod(lo, HALF)
+            root = sb([P, PACK, width], F32, "root%d" % piece)
+            recip[piece] = sb([P, PACK, width], F32, "recip%d" % piece)
+            nc.scalar.activation(root[:], den[h][:, :, at : at + width], ACT.Abs_reciprocal_sqrt, bias=eighth[:], scale=0.5)
+            nc.scalar.activation(recip[piece][:], root[:], ACT.Square)
+
+        w1_q = []
+
+        def prepare_w1(pair, copy):
+            grouped = sb([P, PACK * HALF], BF16, "w1_bf%d" % pair)
+            cast(copy, grouped, w1_raw[pair], 0, HALF)
+            w1_q.append(quantize(grouped, HALF, "w1%d" % pair))
+
+        out_rows = out.rearrange("(u p) j -> p u j", p=P)
+        z_q = {}
+
+        def make_z(piece):
+            lo, width = PIECES[piece]
+            h, at = divmod(lo, HALF)
+            z_bf = sb([P, PACK * width], BF16, "z_bf%d" % piece)
+            nc.vector.tensor_tensor(woven(z_bf[:]), planes(num[h][:, :, at : at + width]), planes(recip[piece][:]), ALU.mult)
+            z_q[piece] = quantize(z_bf, width, "z%d" % piece)
+
+        def finish(piece, copies):
+            lo, width = PIECES[piece]
+            codes, scales = z_q[piece]
+            per_bank = 512 // width
+            for bank in range(PACK // per_bank):
+                o_ps = psum.tile([P, per_bank, width], F32, name="o_ps%d%d" % (piece, bank))
+                for e in range(per_bank):
+                    pair, at = divmod(bank * per_bank + e, 2)
+                    cols = slice(at * P, (at + 1) * P)
+                    nc.tensor.matmul_mx(
+                        out=o_ps[:, e, :],
+                        lhsT=w1_q[pair][0][:, cols].bitcast(FP8X4),
+                        lhsT_scale=w1_q[pair][1][:, cols],
+                        rhs=codes[:].bitcast(FP8X4),
+                        rhs_scale=scales[:],
+                        start=True,
+                        stop=True,
+                    )
+                staged = sb([P, per_bank, width], F32, "staged%d%d" % (piece, bank))
+                copies[bank](staged[:], o_ps[:])
+                nc.sync.dma_start(out_rows[:, bank * per_bank : (bank + 1) * per_bank, lo : lo + width], staged[:])
+
+        square_out(0)
+        gate_out(1, "v")
+        square_out(1)
+        gate_out(0, "v")
+        fetch_power(0, 0)
+        square_out(2)
+        fetch_power(1, 0)
+        square_out(3)
+        gate_out(3, "v")
+        gate_out(2, "s")
+        fetch_power(2, 0)
+        fetch_power(3, 0)
+        for t in range(PACK):
+            add_den(t, 0)
+            fetch_num(t, 0)
+        for t in range(PACK):
+            fetch_power(t, 1)
+        prepare_w1(0, nc.vector.tensor_copy)
+        invert(0)
+        for t in range(PACK):
+            add_den(t, 1)
+        prepare_w1(1, nc.scalar.copy)
+        make_z(0)
+        invert(1)
+        invert(2)
+        for t in range(PACK):
+            fetch_num(t, 1)
+        finish(0, [nc.scalar.copy, nc.scalar.copy])
+        make_z(1)
+        make_z(2)
+        finish(1, [nc.scalar.copy])
+        finish(2, [nc.vector.tensor_copy])

@@ -45,6 +45,8 @@ def tile_picked_featnorm_none_p_kernel(tc, x_words, x_scales, wa, gt, w1, offs, 
         nc.sync.dma_start(offs_sb[:], offs)
         nc.vector.memset(xs[:].bitcast(I32), 0)
         nc.vector.memset(eighth[:], 0.125)
+        warm = sb([P, 1], F32, "warm")
+        nc.scalar.activation(warm[:], eighth[:], ACT.Abs_reciprocal_sqrt)
         scale_rows = x_scales[0].bitcast(I32).rearrange("(q r) c -> r q c", r=4)
         for r in range(4):
             nc.scalar.dma_start(xs[:].bitcast(I32)[r:P:32, :], scale_rows[r])

@@ -1,6 +1,7 @@
 from contextlib import ExitStack
 
 import concourse.mybir as mybir
+from concourse.masks import make_identity
 
 K, T, S, N, H = 512, 2048, 512, 512, 512
 FLOPS = 2 * K * S * H + 2 * S * N * H
@@ -18,8 +19,8 @@ ALU = mybir.AluOpType
 P = 128
 PACK = 4
 HALF = 256
-VECTOR_SHARE = 176
-PIECES = ((0, 256), (256, 128), (384, 128))
+VECTOR_SHARE = 192
+PIECES = ((0, 128), (128, 128), (256, 128), (384, 128))
 
 
 def tile_picked_featnorm_none_p_kernel(tc, x_words, x_scales, wa, gt, w1, offs, fl, out):
@@ -34,7 +35,7 @@ def tile_picked_featnorm_none_p_kernel(tc, x_words, x_scales, wa, gt, w1, offs, 
         offs_sb = keep.tile([P, S // 16], U16, name="offs_sb")
         fl_sb = keep.tile([P, H // 16], U16, name="fl_sb")
         xw = sb([P, T], U32, "xw")
-        xs = sb([P, T], U8, "xs")
+        xs = keep.tile([P, T], U8, name="xs", tag="xs", align_bytes=64)
         gw = sb([P, S], U32, "gw")
         gs = sb([P, S], U8, "gs")
         gate = sb([P, PACK], F32, "gate")
@@ -42,20 +43,23 @@ def tile_picked_featnorm_none_p_kernel(tc, x_words, x_scales, wa, gt, w1, offs, 
         wa_raw = [sb([P, PACK, HALF], F32, "wa_raw%d" % h) for h in range(2)]
         w1_raw = [sb([P, PACK, HALF], F32, "w1_raw%d" % h) for h in range(2)]
 
-        nc.sync.dma_start(offs_sb[:], offs)
-        nc.vector.memset(xs[:].bitcast(I32), 0)
+        nc.vector.memset(xs[:].bitcast(I32)[:, : T // 8], 0)
+        nc.gpsimd.memset(xs[:].bitcast(I32)[:, T // 8 :], 0)
         nc.vector.memset(eighth[:], 0.125)
         warm = sb([P, 1], F32, "warm")
         nc.scalar.activation(warm[:], eighth[:], ACT.Abs_reciprocal_sqrt)
-        scale_rows = x_scales[0].bitcast(I32).rearrange("(q r) c -> r q c", r=4)
-        for r in range(4):
-            nc.scalar.dma_start(xs[:].bitcast(I32)[r:P:32, :], scale_rows[r])
-        nc.sync.dma_start(xw[:].bitcast(I32), x_words[0].rearrange("p n t -> p (n t)").bitcast(I32))
         wa_rows = wa.rearrange("(p j) n -> p j n", j=PACK)
         w1_rows = w1.rearrange("(p j) n -> p j n", j=PACK)
-        for h in range(2):
-            nc.sync.dma_start(wa_raw[h][:], wa_rows[:, :, h * HALF : (h + 1) * HALF])
+        nc.sync.dma_start(wa_raw[0][:], wa_rows[:, :, :HALF])
+        nc.sync.dma_start(offs_sb[:], offs)
         nc.sync.dma_start(gate[:], gt.rearrange("(p t) o -> p (t o)", t=PACK))
+        ident = sb([P, P], F32, "ident")
+        make_identity(nc, ident[:])
+        scale_rows = x_scales[0].bitcast(I32).rearrange("(q r) c -> r q c", r=4)
+        for r in range(4):
+            nc.sync.dma_start(xs[:].bitcast(I32)[r:P:32, :], scale_rows[r])
+        nc.sync.dma_start(xw[:].bitcast(I32), x_words[0].rearrange("p n t -> p (n t)").bitcast(I32))
+        nc.sync.dma_start(wa_raw[1][:], wa_rows[:, :, HALF:])
         nc.sync.dma_start(fl_sb[:], fl)
         for h in range(2):
             nc.sync.dma_start(w1_raw[h][:], w1_rows[:, :, h * HALF : (h + 1) * HALF])
@@ -72,8 +76,8 @@ def tile_picked_featnorm_none_p_kernel(tc, x_words, x_scales, wa, gt, w1, offs, 
         def cast(copy, grouped, raw, lo, hi):
             copy(woven(grouped[:, PACK * lo : PACK * hi]), planes(raw[:, :, lo:hi]))
 
-        def quantize(grouped, width, name):
-            codes = sb([P, width], U32, name + "_codes")
+        def quantize(grouped, width, name, tag=None):
+            codes = keep.tile([P, width], U32, name=name + "_codes", tag=tag or name + "_codes", align_bytes=64)
             scales = sb([P, width], U8, name + "_scales")
             nc.vector.quantize_mx(out=codes[:].bitcast(FP8X4), scales=scales[:], in_=grouped[:])
             return codes, scales
@@ -81,7 +85,9 @@ def tile_picked_featnorm_none_p_kernel(tc, x_words, x_scales, wa, gt, w1, offs, 
         def half(h):
             return slice(h * HALF, (h + 1) * HALF)
 
-        y_ps = [psum.tile([P, H], F32, name="y_ps%d" % t) for t in range(PACK)]
+        y_ps = [psum.tile([P, H], F32, name="y_ps%d" % t, tag="bank%d" % t) for t in range(PACK)]
+        banks = ["bank%d" % b for b in (4, 5, 6, 0, 1)]
+        wa_q = []
         for h in range(2):
             grouped = sb([P, PACK * HALF], BF16, "wa_bf%d" % h)
             if h == 0:
@@ -89,8 +95,10 @@ def tile_picked_featnorm_none_p_kernel(tc, x_words, x_scales, wa, gt, w1, offs, 
             else:
                 cast(nc.vector.tensor_copy, grouped, wa_raw[h], 0, VECTOR_SHARE)
                 cast(nc.scalar.copy, grouped, wa_raw[h], VECTOR_SHARE, HALF)
-            codes, scales = quantize(grouped, HALF, "wa%d" % h)
-            for t in range(PACK):
+            wa_q.append(quantize(grouped, HALF, "wa%d" % h, "xs" if h == 0 else None))
+        for t in range(PACK):
+            for h in range(2):
+                codes, scales = wa_q[h]
                 cols = slice(t * P, (t + 1) * P)
                 nc.tensor.matmul_mx(
                     out=y_ps[t][:, half(h)],
@@ -104,9 +112,15 @@ def tile_picked_featnorm_none_p_kernel(tc, x_words, x_scales, wa, gt, w1, offs, 
 
         gy = [sb([P, H], F32, "gy%d" % t) for t in range(PACK)]
         pw = [sb([P, H], F32, "pw%d" % t) for t in range(PACK)]
-        num = [sb([P, PACK, HALF], F32, "num%d" % h) for h in range(2)]
-        pwf = [sb([P, PACK, HALF], F32, "pwf%d" % h) for h in range(2)]
-        den = [sb([P, PACK, HALF], F32, "den%d" % h) for h in range(2)]
+        REUSED = 1
+        ring = sb([P, 2 * PACK - REUSED, HALF], F32, "num_ring")
+        num = [ring[:, :PACK, :], ring[:, PACK - REUSED :, :]]
+
+        pwf = {(t, 0): sb([P, HALF], F32, "pwf%d0" % t)[:] for t in range(PACK)}
+        EARLY = 4
+        for t in range(EARLY):
+            pwf[t, 1] = sb([P, HALF], F32, "pwf%d1" % t)[:]
+
 
         def square_out(t):
             nc.scalar.activation(pw[t][:], y_ps[t][:], ACT.Square)
@@ -121,47 +135,74 @@ def tile_picked_featnorm_none_p_kernel(tc, x_words, x_scales, wa, gt, w1, offs, 
             return fl_sb[:, h * HALF // 16 : (h + 1) * HALF // 16]
 
         def fetch_power(t, h):
-            nc.scalar.activation(pwf[h][:, t, :], pw[t][:].indirect(entries(h)), ACT.Copy)
+            nc.scalar.activation(pwf[t, h], pw[t][:].indirect(entries(h)), ACT.Copy)
+
+        def fetch_piece(t, piece):
+            at = piece * P - HALF
+            nc.scalar.activation(pwf[t, 1][:, at : at + P], pw[t][:].indirect(fl_sb[:, piece * P // 16 : (piece + 1) * P // 16]), ACT.Copy)
 
         def fetch_num(t, h):
             nc.vector.tensor_tensor(num[h][:, t, :], gy[t][:].indirect(entries(h)), pw[t][:, half(h)], ALU.mult)
 
-        def add_den(t, h):
-            nc.vector.tensor_tensor(den[h][:, t, :], pwf[h][:, t, :], pw[t][:, half(h)], ALU.add)
-
+        den_t = {}
+        roots = {}
+        recip_t = {}
         recip = {}
 
+        def turn_power(piece, t):
+            if t == 0:
+                den_t[piece] = psum.tile([P, PACK, P], F32, name="den_t%d" % piece, tag="bank%d" % (4, 5, 0, 1)[piece])
+            nc.tensor.matmul(den_t[piece][:, t, :], pw[t][:, piece * P : (piece + 1) * P], ident[:], is_transpose=True, start=t == 0, stop=False)
+
+        def turn_fetched(piece, t):
+            h, at = divmod(piece * P, HALF)
+            nc.tensor.matmul(den_t[piece][:, t, :], pwf[t, h][:, at : at + P], ident[:], is_transpose=True, start=False, stop=t == PACK - 1)
+
         def invert(piece):
-            lo, width = PIECES[piece]
-            h, at = divmod(lo, HALF)
-            root = sb([P, PACK, width], F32, "root%d" % piece)
-            recip[piece] = sb([P, PACK, width], F32, "recip%d" % piece)
-            nc.scalar.activation(root[:], den[h][:, :, at : at + width], ACT.Abs_reciprocal_sqrt, bias=eighth[:], scale=0.5)
-            nc.scalar.activation(recip[piece][:], root[:], ACT.Square)
+            roots[piece] = keep.tile([P, PACK, P], F32, name="root%d" % piece, tag="root%d" % piece, align_bytes=64)
+            nc.scalar.activation(roots[piece][:], den_t[piece][:], ACT.Abs_reciprocal_sqrt, bias=eighth[:], scale=0.5)
+
+        def square_root(piece, engine="s"):
+            recip_t[piece] = sb([P, PACK, P], F32, "recip_t%d" % piece)
+            if engine == "s":
+                nc.scalar.activation(recip_t[piece][:], roots[piece][:], ACT.Square)
+            else:
+                nc.vector.tensor_tensor(recip_t[piece][:], roots[piece][:], roots[piece][:], ALU.mult)
+            recip[piece] = psum.tile([P, PACK, P], F32, name="recip%d" % piece, tag="bank%d" % (6, 7, 2, 3)[piece])
+            for t in range(PACK):
+                nc.tensor.transpose(recip[piece][:, t, :], recip_t[piece][:, t, :], ident[:])
 
         w1_q = []
+        w1_bf = []
 
         def prepare_w1(pair, copy):
             grouped = sb([P, PACK * HALF], BF16, "w1_bf%d" % pair)
             cast(copy, grouped, w1_raw[pair], 0, HALF)
-            w1_q.append(quantize(grouped, HALF, "w1%d" % pair))
+            w1_bf.append(grouped)
+
+        def quantize_w1(pair):
+            w1_q.append(quantize(w1_bf[pair], HALF, "w1%d" % pair))
 
         out_rows = out.rearrange("(u p) j -> p u j", p=P)
         z_q = {}
+        z_bfs = {}
 
         def make_z(piece):
             lo, width = PIECES[piece]
             h, at = divmod(lo, HALF)
             z_bf = sb([P, PACK * width], BF16, "z_bf%d" % piece)
             nc.vector.tensor_tensor(woven(z_bf[:]), planes(num[h][:, :, at : at + width]), planes(recip[piece][:]), ALU.mult)
-            z_q[piece] = quantize(z_bf, width, "z%d" % piece)
+            z_bfs[piece] = z_bf
+
+        def quantize_z(piece):
+            z_q[piece] = quantize(z_bfs[piece], PIECES[piece][1], "z%d" % piece)
 
         def finish(piece, copies):
             lo, width = PIECES[piece]
             codes, scales = z_q[piece]
-            per_bank = 512 // width
+            per_bank = PACK // len(copies)
             for bank in range(PACK // per_bank):
-                o_ps = psum.tile([P, per_bank, width], F32, name="o_ps%d%d" % (piece, bank))
+                o_ps = psum.tile([P, per_bank, width], F32, name="o_ps%d%d" % (piece, bank), tag=banks.pop(0))
                 for e in range(per_bank):
                     pair, at = divmod(bank * per_bank + e, 2)
                     cols = slice(at * P, (at + 1) * P)
@@ -180,33 +221,49 @@ def tile_picked_featnorm_none_p_kernel(tc, x_words, x_scales, wa, gt, w1, offs, 
 
         square_out(0)
         gate_out(1, "v")
-        square_out(1)
-        gate_out(0, "v")
         fetch_power(0, 0)
-        square_out(2)
+        gate_out(0, "v")
+        square_out(1)
         fetch_power(1, 0)
-        square_out(3)
         gate_out(3, "v")
-        gate_out(2, "s")
+        square_out(2)
         fetch_power(2, 0)
+        square_out(3)
         fetch_power(3, 0)
+        gate_out(2, "v")
         for t in range(PACK):
-            add_den(t, 0)
-            fetch_num(t, 0)
-        for t in range(PACK):
-            fetch_power(t, 1)
-        prepare_w1(0, nc.vector.tensor_copy)
+            for piece in range(2):
+                turn_power(piece, t)
+            for piece in range(2):
+                turn_fetched(piece, t)
         invert(0)
-        for t in range(PACK):
-            add_den(t, 1)
-        prepare_w1(1, nc.scalar.copy)
-        make_z(0)
         invert(1)
-        invert(2)
+        square_root(0, "s")
+        square_root(1, "v")
         for t in range(PACK):
-            fetch_num(t, 1)
-        finish(0, [nc.scalar.copy, nc.scalar.copy])
+            fetch_num(t, 0)
+        prepare_w1(0, nc.vector.tensor_copy)
+        prepare_w1(1, nc.vector.tensor_copy)
+        quantize_w1(0)
+        quantize_w1(1)
+        make_z(0)
+        quantize_z(0)
         make_z(1)
+        quantize_z(1)
+        for piece in range(2, 4):
+            for t in range(PACK):
+                fetch_piece(t, piece)
+                turn_power(piece, t)
+                turn_fetched(piece, t)
+            invert(piece)
+            square_root(piece, "svss"[piece])
+        for t in reversed(range(PACK)):
+            fetch_num(t, 1)
         make_z(2)
+        quantize_z(2)
+        make_z(3)
+        quantize_z(3)
+        finish(0, [nc.scalar.copy])
         finish(1, [nc.scalar.copy])
-        finish(2, [nc.vector.tensor_copy])
+        finish(2, [nc.scalar.copy])
+        finish(3, [nc.vector.tensor_copy, nc.scalar.copy])

@@ -19,7 +19,7 @@ ALU = mybir.AluOpType
 P = 128
 PACK = 4
 HALF = 256
-VECTOR_SHARE = 192
+VECTOR_SHARE = 160
 PIECES = ((0, 128), (128, 128), (256, 128), (384, 128))
 
 
@@ -110,16 +110,14 @@ def tile_picked_featnorm_none_p_kernel(tc, x_words, x_scales, wa, gt, w1, offs, 
                     stop=True,
                 )
 
-        gy = [sb([P, H], F32, "gy%d" % t) for t in range(PACK)]
+        gy = [sb([P, 2 * H], F32, "gy%d" % t) for t in range(PACK)]
+        for t in range(PACK):
+            nc.vector.memset(gy[t][:, H:], 0.0)
         pw = [sb([P, H], F32, "pw%d" % t) for t in range(PACK)]
-        REUSED = 1
-        ring = sb([P, 2 * PACK - REUSED, HALF], F32, "num_ring")
-        num = [ring[:, :PACK, :], ring[:, PACK - REUSED :, :]]
+        num = sb([P, PACK, H], F32, "num")
 
         pwf = {(t, 0): sb([P, HALF], F32, "pwf%d0" % t)[:] for t in range(PACK)}
-        EARLY = 4
-        for t in range(EARLY):
-            pwf[t, 1] = sb([P, HALF], F32, "pwf%d1" % t)[:]
+        late = {}
 
 
         def square_out(t):
@@ -127,9 +125,9 @@ def tile_picked_featnorm_none_p_kernel(tc, x_words, x_scales, wa, gt, w1, offs, 
 
         def gate_out(t, engine):
             if engine == "s":
-                nc.scalar.activation(gy[t][:], y_ps[t][:], ACT.Copy, scale=gate[:, t : t + 1])
+                nc.scalar.activation(gy[t][:, :H], y_ps[t][:], ACT.Copy, scale=gate[:, t : t + 1])
             else:
-                nc.vector.tensor_scalar(gy[t][:], y_ps[t][:], gate[:, t : t + 1], None, ALU.mult)
+                nc.vector.tensor_scalar(gy[t][:, :H], y_ps[t][:], gate[:, t : t + 1], None, ALU.mult)
 
         def entries(h):
             return fl_sb[:, h * HALF // 16 : (h + 1) * HALF // 16]
@@ -138,11 +136,12 @@ def tile_picked_featnorm_none_p_kernel(tc, x_words, x_scales, wa, gt, w1, offs, 
             nc.scalar.activation(pwf[t, h], pw[t][:].indirect(entries(h)), ACT.Copy)
 
         def fetch_piece(t, piece):
-            at = piece * P - HALF
-            nc.scalar.activation(pwf[t, 1][:, at : at + P], pw[t][:].indirect(fl_sb[:, piece * P // 16 : (piece + 1) * P // 16]), ACT.Copy)
+            if t == 0:
+                late[piece] = keep.tile([P, PACK, P], F32, name="pwf_late%d" % piece, tag="late3" if piece == 3 else "late", align_bytes=64)
+            nc.scalar.activation(late[piece][:, t, :], pw[t][:].indirect(fl_sb[:, piece * P // 16 : (piece + 1) * P // 16]), ACT.Copy)
 
-        def fetch_num(t, h):
-            nc.vector.tensor_tensor(num[h][:, t, :], gy[t][:].indirect(entries(h)), pw[t][:, half(h)], ALU.mult)
+        def fetch_num(t):
+            nc.vector.tensor_tensor(num[:, t, :], gy[t][:].indirect(fl_sb[:]), pw[t][:], ALU.mult)
 
         den_t = {}
         roots = {}
@@ -155,8 +154,8 @@ def tile_picked_featnorm_none_p_kernel(tc, x_words, x_scales, wa, gt, w1, offs, 
             nc.tensor.matmul(den_t[piece][:, t, :], pw[t][:, piece * P : (piece + 1) * P], ident[:], is_transpose=True, start=t == 0, stop=False)
 
         def turn_fetched(piece, t):
-            h, at = divmod(piece * P, HALF)
-            nc.tensor.matmul(den_t[piece][:, t, :], pwf[t, h][:, at : at + P], ident[:], is_transpose=True, start=False, stop=t == PACK - 1)
+            fetched = late[piece][:, t, :] if piece in late else pwf[t, 0][:, piece * P : (piece + 1) * P]
+            nc.tensor.matmul(den_t[piece][:, t, :], fetched, ident[:], is_transpose=True, start=False, stop=t == PACK - 1)
 
         def invert(piece):
             roots[piece] = keep.tile([P, PACK, P], F32, name="root%d" % piece, tag="root%d" % piece, align_bytes=64)
@@ -180,6 +179,9 @@ def tile_picked_featnorm_none_p_kernel(tc, x_words, x_scales, wa, gt, w1, offs, 
             cast(copy, grouped, w1_raw[pair], 0, HALF)
             w1_bf.append(grouped)
 
+        def gpsimd_cast(dst, src):
+            nc.gpsimd.tensor_scalar(dst.rearrange("p c t i -> p c i t"), src.rearrange("p c t i -> p c i t"), 1.0, 0.0, ALU.mult, ALU.add)
+
         def quantize_w1(pair):
             w1_q.append(quantize(w1_bf[pair], HALF, "w1%d" % pair))
 
@@ -189,9 +191,8 @@ def tile_picked_featnorm_none_p_kernel(tc, x_words, x_scales, wa, gt, w1, offs, 
 
         def make_z(piece):
             lo, width = PIECES[piece]
-            h, at = divmod(lo, HALF)
             z_bf = sb([P, PACK * width], BF16, "z_bf%d" % piece)
-            nc.vector.tensor_tensor(woven(z_bf[:]), planes(num[h][:, :, at : at + width]), planes(recip[piece][:]), ALU.mult)
+            nc.vector.tensor_tensor(woven(z_bf[:]), planes(num[:, :, lo : lo + width]), planes(recip[piece][:]), ALU.mult)
             z_bfs[piece] = z_bf
 
         def quantize_z(piece):
@@ -241,9 +242,9 @@ def tile_picked_featnorm_none_p_kernel(tc, x_words, x_scales, wa, gt, w1, offs, 
         square_root(0, "s")
         square_root(1, "v")
         for t in range(PACK):
-            fetch_num(t, 0)
+            fetch_num(t)
         prepare_w1(0, nc.vector.tensor_copy)
-        prepare_w1(1, nc.vector.tensor_copy)
+        prepare_w1(1, gpsimd_cast)
         quantize_w1(0)
         quantize_w1(1)
         make_z(0)
@@ -257,8 +258,6 @@ def tile_picked_featnorm_none_p_kernel(tc, x_words, x_scales, wa, gt, w1, offs, 
                 turn_fetched(piece, t)
             invert(piece)
             square_root(piece, "svss"[piece])
-        for t in reversed(range(PACK)):
-            fetch_num(t, 1)
         make_z(2)
         quantize_z(2)
         make_z(3)

@@ -19,8 +19,13 @@ ALU = mybir.AluOpType
 P = 128
 PACK = 4
 HALF = 256
+PER_COLUMN = 16
+RUN = 4
 VECTOR_SHARE = 160
-PIECES = ((0, 128), (128, 128), (256, 128), (384, 128))
+DEN_BANKS = (4, 5, 0, 1)
+RECIP_BANKS = (6, 7, 2, 3)
+OUT_BANKS = (4, 5, 6)
+LAST_BANKS = (0, 1, 7, 2)
 
 
 def tile_picked_featnorm_none_p_kernel(tc, x_words, x_scales, wa, gt, w1, offs, fl, out):
@@ -29,240 +34,192 @@ def tile_picked_featnorm_none_p_kernel(tc, x_words, x_scales, wa, gt, w1, offs, 
         keep = ctx.enter_context(tc.tile_pool(name="keep", bufs=1))
         psum = ctx.enter_context(tc.psum_pool(name="psum", bufs=1))
 
-        def sb(shape, dtype, name):
-            return keep.tile(shape, dtype, name=name, align_bytes=64)
+        def sbuf(shape, dtype, name, tag=None):
+            return keep.tile(shape, dtype, name=name, tag=tag or name, align_bytes=64)
 
-        offs_sb = keep.tile([P, S // 16], U16, name="offs_sb")
-        fl_sb = keep.tile([P, H // 16], U16, name="fl_sb")
-        xw = sb([P, T], U32, "xw")
-        xs = keep.tile([P, T], U8, name="xs", tag="xs", align_bytes=64)
-        gw = sb([P, S], U32, "gw")
-        gs = sb([P, S], U8, "gs")
-        gate = sb([P, PACK], F32, "gate")
-        eighth = sb([P, 1], F32, "eighth")
-        wa_raw = [sb([P, PACK, HALF], F32, "wa_raw%d" % h) for h in range(2)]
-        w1_raw = [sb([P, PACK, HALF], F32, "w1_raw%d" % h) for h in range(2)]
-
-        nc.vector.memset(xs[:].bitcast(I32)[:, : T // 8], 0)
-        nc.gpsimd.memset(xs[:].bitcast(I32)[:, T // 8 :], 0)
-        nc.vector.memset(eighth[:], 0.125)
-        warm = sb([P, 1], F32, "warm")
-        nc.scalar.activation(warm[:], eighth[:], ACT.Abs_reciprocal_sqrt)
-        wa_rows = wa.rearrange("(p j) n -> p j n", j=PACK)
-        w1_rows = w1.rearrange("(p j) n -> p j n", j=PACK)
-        nc.sync.dma_start(wa_raw[0][:], wa_rows[:, :, :HALF])
-        nc.sync.dma_start(offs_sb[:], offs)
-        nc.sync.dma_start(gate[:], gt.rearrange("(p t) o -> p (t o)", t=PACK))
-        ident = sb([P, P], F32, "ident")
-        make_identity(nc, ident[:])
-        scale_rows = x_scales[0].bitcast(I32).rearrange("(q r) c -> r q c", r=4)
-        for r in range(4):
-            nc.sync.dma_start(xs[:].bitcast(I32)[r:P:32, :], scale_rows[r])
-        nc.sync.dma_start(xw[:].bitcast(I32), x_words[0].rearrange("p n t -> p (n t)").bitcast(I32))
-        nc.sync.dma_start(wa_raw[1][:], wa_rows[:, :, HALF:])
-        nc.sync.dma_start(fl_sb[:], fl)
-        for h in range(2):
-            nc.sync.dma_start(w1_raw[h][:], w1_rows[:, :, h * HALF : (h + 1) * HALF])
-
-        nc.vector.tensor_copy(gs[:].rearrange("p (t m) -> p m t", t=PACK), xs[:].indirect(offs_sb[:]))
-        nc.vector.tensor_copy(gw[:].rearrange("p (t m) -> p m t", t=PACK), xw[:].indirect(offs_sb[:]))
-
-        def woven(flat):
-            return flat.rearrange("p (c i t) -> p c t i", i=4, t=PACK)
-
-        def planes(stack):
-            return stack.rearrange("p t (c i) -> p c t i", i=4)
-
-        def cast(copy, grouped, raw, lo, hi):
-            copy(woven(grouped[:, PACK * lo : PACK * hi]), planes(raw[:, :, lo:hi]))
-
-        def quantize(grouped, width, name, tag=None):
-            codes = keep.tile([P, width], U32, name=name + "_codes", tag=tag or name + "_codes", align_bytes=64)
-            scales = sb([P, width], U8, name + "_scales")
-            nc.vector.quantize_mx(out=codes[:].bitcast(FP8X4), scales=scales[:], in_=grouped[:])
-            return codes, scales
+        def bank(shape, name, number):
+            return psum.tile(shape, F32, name=name, tag="bank%d" % number)
 
         def half(h):
             return slice(h * HALF, (h + 1) * HALF)
 
-        y_ps = [psum.tile([P, H], F32, name="y_ps%d" % t, tag="bank%d" % t) for t in range(PACK)]
-        banks = ["bank%d" % b for b in (4, 5, 6, 0, 1)]
-        wa_q = []
+        def block(b):
+            return slice(b * P, (b + 1) * P)
+
+        offs_sb = keep.tile([P, S // PER_COLUMN], U16, name="offs_sb")
+        fl_sb = keep.tile([P, H // PER_COLUMN], U16, name="fl_sb")
+        table_words = sbuf([P, T], U32, "table_words")
+        table_scales = sbuf([P, T], U8, "table_scales")
+        picked_words = sbuf([P, S], U32, "picked_words")
+        picked_scales = sbuf([P, S], U8, "picked_scales")
+        gate = sbuf([P, PACK], F32, "gate")
+        eighth = sbuf([P, 1], F32, "eighth")
+        wa_raw = [sbuf([P, PACK, HALF], F32, "wa_raw%d" % h) for h in range(2)]
+        w1_raw = [sbuf([P, PACK, HALF], F32, "w1_raw%d" % h) for h in range(2)]
+
+        scale_words = table_scales[:].bitcast(I32)
+        nc.vector.memset(scale_words[:, : T // 8], 0)
+        nc.gpsimd.memset(scale_words[:, T // 8 :], 0)
+        nc.vector.memset(eighth[:], 0.125)
+        warm = sbuf([P, 1], F32, "warm")
+        nc.scalar.activation(warm[:], eighth[:], ACT.Abs_reciprocal_sqrt)
+
+        wa_rows = wa.rearrange("(p j) n -> p j n", j=PACK)
+        w1_rows = w1.rearrange("(p j) n -> p j n", j=PACK)
+        nc.sync.dma_start(wa_raw[0][:], wa_rows[:, :, half(0)])
+        nc.sync.dma_start(offs_sb[:], offs)
+        ident = sbuf([P, P], F32, "ident")
+        make_identity(nc, ident[:])
+        scale_rows = x_scales[0].bitcast(I32).rearrange("(q r) c -> r q c", r=4)
+        for r in range(4):
+            nc.sync.dma_start(scale_words[r:P:32, :], scale_rows[r])
+        nc.sync.dma_start(table_words[:].bitcast(I32), x_words[0].rearrange("p n t -> p (n t)").bitcast(I32))
+        nc.sync.dma_start(wa_raw[1][:], wa_rows[:, :, half(1)])
+        nc.sync.dma_start(gate[:], gt.rearrange("(p t) o -> p (t o)", t=PACK))
+        nc.sync.dma_start(fl_sb[:], fl)
         for h in range(2):
-            grouped = sb([P, PACK * HALF], BF16, "wa_bf%d" % h)
-            if h == 0:
-                cast(nc.scalar.copy, grouped, wa_raw[h], 0, HALF)
-            else:
-                cast(nc.vector.tensor_copy, grouped, wa_raw[h], 0, VECTOR_SHARE)
-                cast(nc.scalar.copy, grouped, wa_raw[h], VECTOR_SHARE, HALF)
-            wa_q.append(quantize(grouped, HALF, "wa%d" % h, "xs" if h == 0 else None))
+            nc.sync.dma_start(w1_raw[h][:], w1_rows[:, :, half(h)])
+
+        def dealt(picked):
+            return picked[:].rearrange("p (t m) -> p m t", t=PACK)
+
+        nc.vector.tensor_copy(dealt(picked_scales), table_scales[:].indirect(offs_sb[:]))
+        nc.vector.tensor_copy(dealt(picked_words), table_words[:].indirect(offs_sb[:]))
+
+        def side_by_side(flat):
+            return flat.rearrange("p (c i t) -> p c t i", i=RUN, t=PACK)
+
+        def row_by_row(stack):
+            return stack.rearrange("p t (c i) -> p c t i", i=RUN)
+
+        def round_columns(copy, rounded, raw, lo, hi):
+            copy(side_by_side(rounded[:, PACK * lo : PACK * hi]), row_by_row(raw[:, :, lo:hi]))
+
+        def quantize(rounded, width, name, codes_tag=None):
+            codes = sbuf([P, width], U32, name + "_codes", codes_tag)
+            scales = sbuf([P, width], U8, name + "_scales")
+            nc.vector.quantize_mx(out=codes[:].bitcast(FP8X4), scales=scales[:], in_=rounded[:])
+            return codes, scales
+
+        def product(target, stationary, columns, moving):
+            nc.tensor.matmul_mx(
+                out=target,
+                lhsT=stationary[0][:, columns].bitcast(FP8X4),
+                lhsT_scale=stationary[1][:, columns],
+                rhs=moving[0][:].bitcast(FP8X4),
+                rhs_scale=moving[1][:],
+                start=True,
+                stop=True,
+            )
+
+        y_ps = [bank([P, H], "y_ps%d" % t, t) for t in range(PACK)]
+        wa_bf0 = sbuf([P, PACK * HALF], BF16, "wa_bf0")
+        round_columns(nc.scalar.copy, wa_bf0, wa_raw[0], 0, HALF)
+        wa_mx = [quantize(wa_bf0, HALF, "wa0", "table_scales")]
+        wa_bf1 = sbuf([P, PACK * HALF], BF16, "wa_bf1")
+        round_columns(nc.vector.tensor_copy, wa_bf1, wa_raw[1], 0, VECTOR_SHARE)
+        round_columns(nc.scalar.copy, wa_bf1, wa_raw[1], VECTOR_SHARE, HALF)
+        wa_mx.append(quantize(wa_bf1, HALF, "wa1"))
         for t in range(PACK):
             for h in range(2):
-                codes, scales = wa_q[h]
-                cols = slice(t * P, (t + 1) * P)
-                nc.tensor.matmul_mx(
-                    out=y_ps[t][:, half(h)],
-                    lhsT=gw[:, cols].bitcast(FP8X4),
-                    lhsT_scale=gs[:, cols],
-                    rhs=codes[:].bitcast(FP8X4),
-                    rhs_scale=scales[:],
-                    start=True,
-                    stop=True,
-                )
+                product(y_ps[t][:, half(h)], (picked_words, picked_scales), block(t), wa_mx[h])
 
-        gy = [sb([P, 2 * H], F32, "gy%d" % t) for t in range(PACK)]
+        gated = [sbuf([P, 2 * H], F32, "gated%d" % t) for t in range(PACK)]
         for t in range(PACK):
-            nc.vector.memset(gy[t][:, H:], 0.0)
-        pw = [sb([P, H], F32, "pw%d" % t) for t in range(PACK)]
-        num = sb([P, PACK, H], F32, "num")
+            nc.vector.memset(gated[t][:, H:], 0.0)
+        power = [sbuf([P, H], F32, "power%d" % t) for t in range(PACK)]
+        numer = sbuf([P, PACK, H], F32, "numer")
+        fetched_early = [sbuf([P, HALF], F32, "fetched_early%d" % t) for t in range(PACK)]
 
-        pwf = {(t, 0): sb([P, HALF], F32, "pwf%d0" % t)[:] for t in range(PACK)}
-        late = {}
+        def fetch_power(target, t, lo, hi):
+            entries = fl_sb[:, lo // PER_COLUMN : hi // PER_COLUMN]
+            nc.scalar.activation(target, power[t][:].indirect(entries), ACT.Copy)
 
+        for t in range(PACK):
+            other = t ^ 1
+            nc.scalar.activation(power[t][:], y_ps[t][:], ACT.Square)
+            nc.vector.tensor_scalar(gated[other][:, :H], y_ps[other][:], gate[:, other : other + 1], None, ALU.mult)
+            fetch_power(fetched_early[t][:], t, 0, HALF)
 
-        def square_out(t):
-            nc.scalar.activation(pw[t][:], y_ps[t][:], ACT.Square)
-
-        def gate_out(t, engine):
-            if engine == "s":
-                nc.scalar.activation(gy[t][:, :H], y_ps[t][:], ACT.Copy, scale=gate[:, t : t + 1])
-            else:
-                nc.vector.tensor_scalar(gy[t][:, :H], y_ps[t][:], gate[:, t : t + 1], None, ALU.mult)
-
-        def entries(h):
-            return fl_sb[:, h * HALF // 16 : (h + 1) * HALF // 16]
-
-        def fetch_power(t, h):
-            nc.scalar.activation(pwf[t, h], pw[t][:].indirect(entries(h)), ACT.Copy)
-
-        def fetch_piece(t, piece):
-            if t == 0:
-                late[piece] = keep.tile([P, PACK, P], F32, name="pwf_late%d" % piece, tag="late3" if piece == 3 else "late", align_bytes=64)
-            nc.scalar.activation(late[piece][:, t, :], pw[t][:].indirect(fl_sb[:, piece * P // 16 : (piece + 1) * P // 16]), ACT.Copy)
-
-        def fetch_num(t):
-            nc.vector.tensor_tensor(num[:, t, :], gy[t][:].indirect(fl_sb[:]), pw[t][:], ALU.mult)
-
-        den_t = {}
-        roots = {}
-        recip_t = {}
-        recip = {}
+        den, root, recip = {}, {}, {}
 
         def turn_power(piece, t):
             if t == 0:
-                den_t[piece] = psum.tile([P, PACK, P], F32, name="den_t%d" % piece, tag="bank%d" % (4, 5, 0, 1)[piece])
-            nc.tensor.matmul(den_t[piece][:, t, :], pw[t][:, piece * P : (piece + 1) * P], ident[:], is_transpose=True, start=t == 0, stop=False)
+                den[piece] = bank([P, PACK, P], "den%d" % piece, DEN_BANKS[piece])
+            nc.tensor.matmul(den[piece][:, t, :], power[t][:, block(piece)], ident[:], is_transpose=True, start=t == 0, stop=False)
 
-        def turn_fetched(piece, t):
-            fetched = late[piece][:, t, :] if piece in late else pwf[t, 0][:, piece * P : (piece + 1) * P]
-            nc.tensor.matmul(den_t[piece][:, t, :], fetched, ident[:], is_transpose=True, start=False, stop=t == PACK - 1)
+        def add_fetched(piece, t, fetched):
+            nc.tensor.matmul(den[piece][:, t, :], fetched, ident[:], is_transpose=True, start=False, stop=t == PACK - 1)
 
-        def invert(piece):
-            roots[piece] = keep.tile([P, PACK, P], F32, name="root%d" % piece, tag="root%d" % piece, align_bytes=64)
-            nc.scalar.activation(roots[piece][:], den_t[piece][:], ACT.Abs_reciprocal_sqrt, bias=eighth[:], scale=0.5)
+        def inverse_root(piece):
+            root[piece] = sbuf([P, PACK, P], F32, "root%d" % piece)
+            nc.scalar.activation(root[piece][:], den[piece][:], ACT.Abs_reciprocal_sqrt, bias=eighth[:], scale=0.5)
 
-        def square_root(piece, engine="s"):
-            recip_t[piece] = sb([P, PACK, P], F32, "recip_t%d" % piece)
-            if engine == "s":
-                nc.scalar.activation(recip_t[piece][:], roots[piece][:], ACT.Square)
-            else:
-                nc.vector.tensor_tensor(recip_t[piece][:], roots[piece][:], roots[piece][:], ALU.mult)
-            recip[piece] = psum.tile([P, PACK, P], F32, name="recip%d" % piece, tag="bank%d" % (6, 7, 2, 3)[piece])
+        def square_on_scalar(target, source):
+            nc.scalar.activation(target, source, ACT.Square)
+
+        def square_on_vector(target, source):
+            nc.vector.tensor_tensor(target, source, source, ALU.mult)
+
+        def reciprocal(piece, square):
+            turned = sbuf([P, PACK, P], F32, "recip_turned%d" % piece)
+            square(turned[:], root[piece][:])
+            recip[piece] = bank([P, PACK, P], "recip%d" % piece, RECIP_BANKS[piece])
             for t in range(PACK):
-                nc.tensor.transpose(recip[piece][:, t, :], recip_t[piece][:, t, :], ident[:])
+                nc.tensor.transpose(recip[piece][:, t, :], turned[:, t, :], ident[:])
 
-        w1_q = []
-        w1_bf = []
+        for t in range(PACK):
+            for piece in range(2):
+                turn_power(piece, t)
+            for piece in range(2):
+                add_fetched(piece, t, fetched_early[t][:, block(piece)])
+        inverse_root(0)
+        inverse_root(1)
+        reciprocal(0, square_on_scalar)
+        reciprocal(1, square_on_vector)
+        for t in range(PACK):
+            nc.vector.tensor_tensor(numer[:, t, :], gated[t][:].indirect(fl_sb[:]), power[t][:], ALU.mult)
 
-        def prepare_w1(pair, copy):
-            grouped = sb([P, PACK * HALF], BF16, "w1_bf%d" % pair)
-            cast(copy, grouped, w1_raw[pair], 0, HALF)
-            w1_bf.append(grouped)
+        w1_bf0 = sbuf([P, PACK * HALF], BF16, "w1_bf0")
+        round_columns(nc.vector.tensor_copy, w1_bf0, w1_raw[0], 0, HALF)
+        w1_bf1 = sbuf([P, PACK * HALF], BF16, "w1_bf1")
+        nc.gpsimd.tensor_scalar(
+            w1_bf1[:].rearrange("p (c t) -> p c t", t=PACK), w1_raw[1][:].rearrange("p t c -> p c t"), 1.0, 0.0, ALU.mult, ALU.add
+        )
+        w1_mx = [quantize(w1_bf0, HALF, "w10"), quantize(w1_bf1, HALF, "w11")]
 
-        def gpsimd_cast(dst, src):
-            nc.gpsimd.tensor_scalar(dst.rearrange("p c t i -> p c i t"), src.rearrange("p c t i -> p c i t"), 1.0, 0.0, ALU.mult, ALU.add)
-
-        def quantize_w1(pair):
-            w1_q.append(quantize(w1_bf[pair], HALF, "w1%d" % pair))
-
-        out_rows = out.rearrange("(u p) j -> p u j", p=P)
-        z_q = {}
-        z_bfs = {}
+        z_mx = {}
 
         def make_z(piece):
-            lo, width = PIECES[piece]
-            z_bf = sb([P, PACK * width], BF16, "z_bf%d" % piece)
-            nc.vector.tensor_tensor(woven(z_bf[:]), planes(num[:, :, lo : lo + width]), planes(recip[piece][:]), ALU.mult)
-            z_bfs[piece] = z_bf
+            z_bf = sbuf([P, PACK * P], BF16, "z_bf%d" % piece)
+            nc.vector.tensor_tensor(side_by_side(z_bf[:]), row_by_row(numer[:, :, block(piece)]), row_by_row(recip[piece][:]), ALU.mult)
+            z_mx[piece] = quantize(z_bf, P, "z%d" % piece)
 
-        def quantize_z(piece):
-            z_q[piece] = quantize(z_bfs[piece], PIECES[piece][1], "z%d" % piece)
-
-        def finish(piece, copies):
-            lo, width = PIECES[piece]
-            codes, scales = z_q[piece]
-            per_bank = PACK // len(copies)
-            for bank in range(PACK // per_bank):
-                o_ps = psum.tile([P, per_bank, width], F32, name="o_ps%d%d" % (piece, bank), tag=banks.pop(0))
-                for e in range(per_bank):
-                    pair, at = divmod(bank * per_bank + e, 2)
-                    cols = slice(at * P, (at + 1) * P)
-                    nc.tensor.matmul_mx(
-                        out=o_ps[:, e, :],
-                        lhsT=w1_q[pair][0][:, cols].bitcast(FP8X4),
-                        lhsT_scale=w1_q[pair][1][:, cols],
-                        rhs=codes[:].bitcast(FP8X4),
-                        rhs_scale=scales[:],
-                        start=True,
-                        stop=True,
-                    )
-                staged = sb([P, per_bank, width], F32, "staged%d%d" % (piece, bank))
-                copies[bank](staged[:], o_ps[:])
-                nc.sync.dma_start(out_rows[:, bank * per_bank : (bank + 1) * per_bank, lo : lo + width], staged[:])
-
-        square_out(0)
-        gate_out(1, "v")
-        fetch_power(0, 0)
-        gate_out(0, "v")
-        square_out(1)
-        fetch_power(1, 0)
-        gate_out(3, "v")
-        square_out(2)
-        fetch_power(2, 0)
-        square_out(3)
-        fetch_power(3, 0)
-        gate_out(2, "v")
-        for t in range(PACK):
-            for piece in range(2):
-                turn_power(piece, t)
-            for piece in range(2):
-                turn_fetched(piece, t)
-        invert(0)
-        invert(1)
-        square_root(0, "s")
-        square_root(1, "v")
-        for t in range(PACK):
-            fetch_num(t)
-        prepare_w1(0, nc.vector.tensor_copy)
-        prepare_w1(1, gpsimd_cast)
-        quantize_w1(0)
-        quantize_w1(1)
         make_z(0)
-        quantize_z(0)
         make_z(1)
-        quantize_z(1)
         for piece in range(2, 4):
+            fetched_late = sbuf([P, PACK, P], F32, "fetched_late%d" % piece)
             for t in range(PACK):
-                fetch_piece(t, piece)
+                fetch_power(fetched_late[:, t, :], t, piece * P, (piece + 1) * P)
                 turn_power(piece, t)
-                turn_fetched(piece, t)
-            invert(piece)
-            square_root(piece, "svss"[piece])
+                add_fetched(piece, t, fetched_late[:, t, :])
+            inverse_root(piece)
+            reciprocal(piece, square_on_scalar)
         make_z(2)
-        quantize_z(2)
         make_z(3)
-        quantize_z(3)
-        finish(0, [nc.scalar.copy])
-        finish(1, [nc.scalar.copy])
-        finish(2, [nc.scalar.copy])
-        finish(3, [nc.vector.tensor_copy, nc.scalar.copy])
+
+        out_rows = out.rearrange("(u p) j -> p u j", p=P)
+        for piece in range(3):
+            o_ps = bank([P, PACK, P], "o_ps%d" % piece, OUT_BANKS[piece])
+            for u in range(PACK):
+                product(o_ps[:, u, :], w1_mx[u // 2], block(u % 2), z_mx[piece])
+            staged = sbuf([P, PACK, P], F32, "staged%d" % piece)
+            nc.scalar.copy(staged[:], o_ps[:])
+            nc.sync.dma_start(out_rows[:, :, block(piece)], staged[:])
+        for h in range(2):
+            staged = sbuf([P, 2, P], F32, "staged_last%d" % h)
+            for e, copy in enumerate((nc.vector.tensor_copy, nc.scalar.copy)):
+                o_ps = bank([P, P], "o_last%d%d" % (h, e), LAST_BANKS[2 * h + e])
+                product(o_ps[:], w1_mx[h], block(e), z_mx[3])
+                copy(staged[:, e, :], o_ps[:])
+            nc.sync.dma_start(out_rows[:, 2 * h : 2 * h + 2, block(3)], staged[:])

from contextlib import ExitStack

import concourse.mybir as mybir
from concourse.masks import make_identity

K, T, S, N, H = 512, 2048, 512, 512, 512
FLOPS = 2 * K * S * H + 2 * S * N * H

F32 = mybir.dt.float32
BF16 = mybir.dt.bfloat16
I32 = mybir.dt.int32
U32 = mybir.dt.uint32
U16 = mybir.dt.uint16
U8 = mybir.dt.uint8
FP8X4 = mybir.dt.float8_e4m3fn_x4
ACT = mybir.ActivationFunctionType
ALU = mybir.AluOpType

P = 128
PACK = 4
HALF = 256
PER_COLUMN = 16
RUN = 4
VECTOR_SHARE = 160
DEN_BANKS = (4, 5, 0, 1)
RECIP_BANKS = (6, 7, 2, 3)
OUT_BANKS = (4, 5, 6)
LAST_BANKS = (0, 1, 7, 2)


def tile_picked_featnorm_none_p_kernel(tc, x_words, x_scales, wa, gt, w1, offs, fl, out):
    nc = tc.nc
    with ExitStack() as ctx:
        keep = ctx.enter_context(tc.tile_pool(name="keep", bufs=1))
        psum = ctx.enter_context(tc.psum_pool(name="psum", bufs=1))

        def sbuf(shape, dtype, name, tag=None):
            return keep.tile(shape, dtype, name=name, tag=tag or name, align_bytes=64)

        def bank(shape, name, number):
            return psum.tile(shape, F32, name=name, tag="bank%d" % number)

        def half(h):
            return slice(h * HALF, (h + 1) * HALF)

        def block(b):
            return slice(b * P, (b + 1) * P)

        offs_sb = keep.tile([P, S // PER_COLUMN], U16, name="offs_sb")
        fl_sb = keep.tile([P, H // PER_COLUMN], U16, name="fl_sb")
        table_words = sbuf([P, T], U32, "table_words")
        table_scales = sbuf([P, T], U8, "table_scales")
        picked_words = sbuf([P, S], U32, "picked_words")
        picked_scales = sbuf([P, S], U8, "picked_scales")
        gate = sbuf([P, PACK], F32, "gate")
        eighth = sbuf([P, 1], F32, "eighth")
        wa_raw = [sbuf([P, PACK, HALF], F32, "wa_raw%d" % h) for h in range(2)]
        w1_raw = [sbuf([P, PACK, HALF], F32, "w1_raw%d" % h) for h in range(2)]

        scale_words = table_scales[:].bitcast(I32)
        nc.vector.memset(scale_words[:, : T // 8], 0)
        nc.gpsimd.memset(scale_words[:, T // 8 :], 0)
        nc.vector.memset(eighth[:], 0.125)
        warm = sbuf([P, 1], F32, "warm")
        nc.scalar.activation(warm[:], eighth[:], ACT.Abs_reciprocal_sqrt)

        wa_rows = wa.rearrange("(p j) n -> p j n", j=PACK)
        w1_rows = w1.rearrange("(p j) n -> p j n", j=PACK)
        nc.sync.dma_start(wa_raw[0][:], wa_rows[:, :, half(0)])
        nc.sync.dma_start(offs_sb[:], offs)
        ident = sbuf([P, P], F32, "ident")
        make_identity(nc, ident[:])
        scale_rows = x_scales[0].bitcast(I32).rearrange("(q r) c -> r q c", r=4)
        for r in range(4):
            nc.sync.dma_start(scale_words[r:P:32, :], scale_rows[r])
        nc.sync.dma_start(table_words[:].bitcast(I32), x_words[0].rearrange("p n t -> p (n t)").bitcast(I32))
        nc.sync.dma_start(wa_raw[1][:], wa_rows[:, :, half(1)])
        nc.sync.dma_start(gate[:], gt.rearrange("(p t) o -> p (t o)", t=PACK))
        nc.sync.dma_start(fl_sb[:], fl)
        for h in range(2):
            nc.sync.dma_start(w1_raw[h][:], w1_rows[:, :, half(h)])

        def dealt(picked):
            return picked[:].rearrange("p (t m) -> p m t", t=PACK)

        nc.vector.tensor_copy(dealt(picked_scales), table_scales[:].indirect(offs_sb[:]))
        nc.vector.tensor_copy(dealt(picked_words), table_words[:].indirect(offs_sb[:]))

        def side_by_side(flat):
            return flat.rearrange("p (c i t) -> p c t i", i=RUN, t=PACK)

        def row_by_row(stack):
            return stack.rearrange("p t (c i) -> p c t i", i=RUN)

        def round_columns(copy, rounded, raw, lo, hi):
            copy(side_by_side(rounded[:, PACK * lo : PACK * hi]), row_by_row(raw[:, :, lo:hi]))

        def quantize(rounded, width, name, codes_tag=None):
            codes = sbuf([P, width], U32, name + "_codes", codes_tag)
            scales = sbuf([P, width], U8, name + "_scales")
            nc.vector.quantize_mx(out=codes[:].bitcast(FP8X4), scales=scales[:], in_=rounded[:])
            return codes, scales

        def product(target, stationary, columns, moving):
            nc.tensor.matmul_mx(
                out=target,
                lhsT=stationary[0][:, columns].bitcast(FP8X4),
                lhsT_scale=stationary[1][:, columns],
                rhs=moving[0][:].bitcast(FP8X4),
                rhs_scale=moving[1][:],
                start=True,
                stop=True,
            )

        y_ps = [bank([P, H], "y_ps%d" % t, t) for t in range(PACK)]
        wa_bf0 = sbuf([P, PACK * HALF], BF16, "wa_bf0")
        round_columns(nc.scalar.copy, wa_bf0, wa_raw[0], 0, HALF)
        wa_mx = [quantize(wa_bf0, HALF, "wa0", "table_scales")]
        wa_bf1 = sbuf([P, PACK * HALF], BF16, "wa_bf1")
        round_columns(nc.vector.tensor_copy, wa_bf1, wa_raw[1], 0, VECTOR_SHARE)
        round_columns(nc.scalar.copy, wa_bf1, wa_raw[1], VECTOR_SHARE, HALF)
        wa_mx.append(quantize(wa_bf1, HALF, "wa1"))
        for t in range(PACK):
            for h in range(2):
                product(y_ps[t][:, half(h)], (picked_words, picked_scales), block(t), wa_mx[h])

        gated = [sbuf([P, 2 * H], F32, "gated%d" % t) for t in range(PACK)]
        for t in range(PACK):
            nc.vector.memset(gated[t][:, H:], 0.0)
        power = [sbuf([P, H], F32, "power%d" % t) for t in range(PACK)]
        numer = sbuf([P, PACK, H], F32, "numer")
        fetched_early = [sbuf([P, HALF], F32, "fetched_early%d" % t) for t in range(PACK)]

        def fetch_power(target, t, lo, hi):
            entries = fl_sb[:, lo // PER_COLUMN : hi // PER_COLUMN]
            nc.scalar.activation(target, power[t][:].indirect(entries), ACT.Copy)

        for t in range(PACK):
            other = t ^ 1
            nc.scalar.activation(power[t][:], y_ps[t][:], ACT.Square)
            nc.vector.tensor_scalar(gated[other][:, :H], y_ps[other][:], gate[:, other : other + 1], None, ALU.mult)
            fetch_power(fetched_early[t][:], t, 0, HALF)

        den, root, recip = {}, {}, {}

        def turn_power(piece, t):
            if t == 0:
                den[piece] = bank([P, PACK, P], "den%d" % piece, DEN_BANKS[piece])
            nc.tensor.matmul(den[piece][:, t, :], power[t][:, block(piece)], ident[:], is_transpose=True, start=t == 0, stop=False)

        def add_fetched(piece, t, fetched):
            nc.tensor.matmul(den[piece][:, t, :], fetched, ident[:], is_transpose=True, start=False, stop=t == PACK - 1)

        def inverse_root(piece):
            root[piece] = sbuf([P, PACK, P], F32, "root%d" % piece)
            nc.scalar.activation(root[piece][:], den[piece][:], ACT.Abs_reciprocal_sqrt, bias=eighth[:], scale=0.5)

        def square_on_scalar(target, source):
            nc.scalar.activation(target, source, ACT.Square)

        def square_on_vector(target, source):
            nc.vector.tensor_tensor(target, source, source, ALU.mult)

        def reciprocal(piece, square):
            turned = sbuf([P, PACK, P], F32, "recip_turned%d" % piece)
            square(turned[:], root[piece][:])
            recip[piece] = bank([P, PACK, P], "recip%d" % piece, RECIP_BANKS[piece])
            for t in range(PACK):
                nc.tensor.transpose(recip[piece][:, t, :], turned[:, t, :], ident[:])

        for t in range(PACK):
            for piece in range(2):
                turn_power(piece, t)
            for piece in range(2):
                add_fetched(piece, t, fetched_early[t][:, block(piece)])
        inverse_root(0)
        inverse_root(1)
        reciprocal(0, square_on_scalar)
        reciprocal(1, square_on_vector)
        for t in range(PACK):
            nc.vector.tensor_tensor(numer[:, t, :], gated[t][:].indirect(fl_sb[:]), power[t][:], ALU.mult)

        w1_bf0 = sbuf([P, PACK * HALF], BF16, "w1_bf0")
        round_columns(nc.vector.tensor_copy, w1_bf0, w1_raw[0], 0, HALF)
        w1_bf1 = sbuf([P, PACK * HALF], BF16, "w1_bf1")
        nc.gpsimd.tensor_scalar(
            w1_bf1[:].rearrange("p (c t) -> p c t", t=PACK), w1_raw[1][:].rearrange("p t c -> p c t"), 1.0, 0.0, ALU.mult, ALU.add
        )
        w1_mx = [quantize(w1_bf0, HALF, "w10"), quantize(w1_bf1, HALF, "w11")]

        z_mx = {}

        def make_z(piece):
            z_bf = sbuf([P, PACK * P], BF16, "z_bf%d" % piece)
            nc.vector.tensor_tensor(side_by_side(z_bf[:]), row_by_row(numer[:, :, block(piece)]), row_by_row(recip[piece][:]), ALU.mult)
            z_mx[piece] = quantize(z_bf, P, "z%d" % piece)

        make_z(0)
        make_z(1)
        for piece in range(2, 4):
            fetched_late = sbuf([P, PACK, P], F32, "fetched_late%d" % piece)
            for t in range(PACK):
                fetch_power(fetched_late[:, t, :], t, piece * P, (piece + 1) * P)
                turn_power(piece, t)
                add_fetched(piece, t, fetched_late[:, t, :])
            inverse_root(piece)
            reciprocal(piece, square_on_scalar)
        make_z(2)
        make_z(3)

        out_rows = out.rearrange("(u p) j -> p u j", p=P)
        for piece in range(3):
            o_ps = bank([P, PACK, P], "o_ps%d" % piece, OUT_BANKS[piece])
            for u in range(PACK):
                product(o_ps[:, u, :], w1_mx[u // 2], block(u % 2), z_mx[piece])
            staged = sbuf([P, PACK, P], F32, "staged%d" % piece)
            nc.scalar.copy(staged[:], o_ps[:])
            nc.sync.dma_start(out_rows[:, :, block(piece)], staged[:])
        for h in range(2):
            staged = sbuf([P, 2, P], F32, "staged_last%d" % h)
            for e, copy in enumerate((nc.vector.tensor_copy, nc.scalar.copy)):
                o_ps = bank([P, P], "o_last%d%d" % (h, e), LAST_BANKS[2 * h + e])
                product(o_ps[:], w1_mx[h], block(e), z_mx[3])
                copy(staged[:, e, :], o_ps[:])
            nc.sync.dma_start(out_rows[:, 2 * h : 2 * h + 2, block(3)], staged[:])
